import numpy as np, ml_dtypes
CORES = [1,9,17,25,102,110,118,126]
N = 8
ROOT = 6
WIDTHS = [8,4,1,1,1,4,8,8]
XW = 8
def setup_inputs(rng):
    return {"x": rng.standard_normal((N, 128, XW), dtype=np.float32).astype(ml_dtypes.bfloat16)}
def reference(x):
    g = np.concatenate([x[r][:, :WIDTHS[r]] for r in range(N)], axis=1)
    y = np.full((N, 128, g.shape[1]), np.nan, x.dtype)
    y[ROOT] = g
    return {"y": y}

SCRATCH = {
    "stage": ("sbuf", [128, 8], "bfloat16"),
    "relay": ("sbuf", [128, 8], "bfloat16"),
    "land": ("sbuf", [128, 35], "bfloat16"),
}
SEMAPHORES = ["loaded", "arrived", "sent", "stored"]

OFF_CHIP_ENGINES = 8
ON_CHIP_ENGINES = 16


def plan(T, topo):
    widths = T.tables["WIDTHS"]
    cores = list(T.cores)
    root = cores[T.tables["ROOT"]] if "ROOT" in T.tables else cores[T.root]
    offs = [sum(widths[:r]) for r in range(len(widths))]
    port = {0: 0, 1: 0}
    blocked = []
    for r, c in enumerate(cores):
        if c == root:
            continue
        if not topo.may_write(c, root):
            blocked.append(r)
        elif topo.chip(c) != topo.chip(root) and not topo.mates(topo.chip(c), topo.chip(root)):
            port[topo.die(c)] += widths[r]
    helpers = {}
    for r in sorted(blocked, key=lambda q: (-widths[q], q)):
        first = topo.chip(cores[r]) * topo.CORES_PER_CHIP
        free = [k for k in range(first, first + topo.CORES_PER_CHIP)
                if k not in cores and topo.may_write(k, root)]
        h = min(free, key=lambda k: (port[topo.die(k)], k))
        helpers[r] = h
        port[topo.die(h)] += widths[r]
    return root, offs, helpers


def send(g, T, topo, src, dst, out_ap, in_ap):
    rid, pid, _se = topo.addr(dst)
    g.remote_dma(out_ap, in_ap, remote_sem=T.sem.arrived, local_sem=T.sem.sent, pid=pid, routing_id=rid,
                 dma_engine_mask=topo.mask(src, dst))
    return ON_CHIP_ENGINES if topo.chip(src) == topo.chip(dst) else OFF_CHIP_ENGINES


def rank_program(g, core, T, topo):
    widths = T.tables["WIDTHS"]
    root, offs, helpers = plan(T, topo)
    rank = T.rank_of(core)

    if rank is None:
        for r, h in helpers.items():
            if h == core:
                w, o = widths[r], offs[r]
                g.wait_ge(T.sem.arrived, ON_CHIP_ENGINES)
                n = send(g, T, topo, core, root, T.land[:, o:o + w], T.relay[:, 0:w])
                g.wait_ge(T.sem.sent, n)
        return

    w, o = widths[rank], offs[rank]

    if core == root:
        g.sync.dma_start(T.land[:, o:o + w], T.x[:, 0:w]).then_inc(T.sem.arrived, 16)
        total = 16
        for r, c in enumerate(T.cores):
            if c != root:
                last = helpers.get(r, c)
                total += ON_CHIP_ENGINES if topo.chip(last) == topo.chip(root) else OFF_CHIP_ENGINES
        g.sync.wait_ge(T.sem.arrived, total)
        g.sync.dma_start(T.y[:, :], T.land[:, :]).then_inc(T.sem.stored, 16)
        g.sync.wait_ge(T.sem.stored, 16)
        return

    lw = max(w, 2)
    g.sync.dma_start(T.stage[:, 0:lw], T.x[:, 0:lw]).then_inc(T.sem.loaded, 16)
    g.wait_ge(T.sem.loaded, 16)
    if rank in helpers:
        n = send(g, T, topo, core, helpers[rank], T.relay[:, 0:w], T.stage[:, 0:w])
    else:
        n = send(g, T, topo, core, root, T.land[:, o:o + w], T.stage[:, 0:w])
    g.wait_ge(T.sem.sent, n)
